import numpy as np
import ml_dtypes


def mxq(x, axis, fmt="e4m3"):
    dtype, down = {"e4m3": (ml_dtypes.float8_e4m3fn, 7), "e5m2": (ml_dtypes.float8_e5m2, 14)}[fmt]
    v = np.moveaxis(np.asarray(x, np.float32).astype(ml_dtypes.bfloat16).astype(np.float64), axis, -1)
    blocks = v.reshape(v.shape[:-1] + (-1, 32))
    amax = np.abs(blocks).max(-1, keepdims=True)
    byte = np.maximum(np.where(amax > 0, np.frexp(amax)[1] - 1 + 127, 0) - down, 1)
    scale = np.exp2(byte - 127.0)
    codes = (blocks / scale).astype(np.float32).astype(dtype).astype(np.float64)
    return np.moveaxis((codes * scale).reshape(v.shape), -1, axis)


WIDE = False


def mx_kscale(k):
    if not WIDE:
        return np.ones(k)
    levels = np.array([10, -10, 5, -5, 0])
    if k % 512:
        return np.exp2(np.random.permutation(np.resize(levels, k // 32))).repeat(32)
    a = np.empty((k // 512, 16))
    for p in range(k // 512):
        a[p, :8] = np.random.permutation(np.resize(levels, 8))
        for g in range(8):
            far = levels[np.abs(levels - a[p, g]) >= 10]
            a[p, g + 8] = far[np.random.randint(len(far))]
    return np.exp2(a.ravel()).repeat(32)


def f64(x):
    return np.asarray(x).astype(np.float64)


def striped(idx):
    return np.tile(idx.reshape(-1, 16).T, (8, 1)).astype(np.uint16)


def unstriped(offs):
    return offs[:16].T.reshape(-1).astype(np.int64)


def pack_weight(w):
    k, n = w.shape
    w = f64(np.asarray(w, np.float32).astype(ml_dtypes.bfloat16)).reshape(k // 32, 32, n)
    amax = np.abs(w).max(1)
    byte = np.clip(np.where(amax > 0, np.frexp(amax)[1] - 1 + 127 - 7, 1), 1, 254)
    scaled = (w * np.exp2(127.0 - byte)[:, None, :]).reshape(k, n).astype(np.float32)
    words = np.ascontiguousarray(scaled.reshape(k // 512, 128, 4, n).transpose(0, 1, 3, 2)).astype(ml_dtypes.float8_e4m3fn).view(np.uint8)
    return words, np.ascontiguousarray(byte.astype(np.uint8).reshape(k // 512, 16, n))


def unpack_weight(words, scales):
    g, p, n, _ = words.shape
    vals = np.ascontiguousarray(words).view(ml_dtypes.float8_e4m3fn).astype(np.float64) * np.repeat(np.exp2(scales.astype(np.float64) - 127.0), 8, axis=1)[..., None]
    return vals.transpose(0, 1, 3, 2).reshape(g * 512, n)


K, T, S, N, D = 512, 2048, 512, 128, 3
P = 2 ** 7


def setup_inputs():
    n = np.random.standard_normal
    s = mx_kscale(K)[:, None]
    packed_xT = pack_weight(n((K, T)) * s)
    return {
        "x_words": packed_xT[0],
        "x_scales": packed_xT[1],
        "w1": (n((K, N)) / np.sqrt(K) / s).astype(np.float32),
        "sus": (np.random.uniform(0.3, 0.95, (N, S))).astype(np.float32),
        "inf": (np.random.uniform(0.0, 0.3, (N, S)) ** 1.5).astype(np.float32),
        "lat": (np.random.uniform(0.0, 0.2, (N, S))).astype(np.float32),
        "mob": (np.tile(np.random.uniform(0.05, 0.3, (D, 1, S)), (1, P, 1))).astype(np.float32),
        "rate": (np.random.uniform(0.1, 0.6, (N, 1))).astype(np.float32),
        "offs": striped(np.random.permutation(T)[:S]),
        "pos1": striped(np.random.permutation(S)[:S]),
        "pos2": striped(np.random.permutation(S)[:S]),
        "pos3": striped(np.random.permutation(S)[:S]),
    }


def reference(x_words, x_scales, w1, sus, inf, lat, mob, rate, offs, pos1, pos2, pos3):
    xq = unpack_weight(x_words, x_scales)[:, unstriped(offs)]
    y = mxq(f64(w1), 0, "e4m3").T @ xq
    beta = 0.6 * (np.log(np.exp(y) + 1.0))
    bi = beta * f64(inf)
    force = bi + beta * (bi[:, unstriped(pos1)] * f64(mob)[0, :1] + bi[:, unstriped(pos2)] * f64(mob)[1, :1] + bi[:, unstriped(pos3)] * f64(mob)[2, :1])
    newi = f64(sus) * (-1.0 * np.exp(-1.0 * force) + 1.0)
    s2 = f64(sus) - newi
    i2 = f64(inf) + f64(rate) * f64(lat) - (0.3 * f64(inf))
    bj = beta * i2
    return s2 * (-1.0 * (np.exp(-1.0 * (bj + beta * (bj[:, unstriped(pos1)] * f64(mob)[0, :1] + bj[:, unstriped(pos2)] * f64(mob)[1, :1] + bj[:, unstriped(pos3)] * f64(mob)[2, :1])))) + 1.0)

@@ -1,0 +1,195 @@
+from contextlib import ExitStack
+
+import concourse.mybir as mybir
+from concourse.masks import make_identity
+
+K, T, S, N, D = 512, 2048, 512, 128, 3
+P = 128
+FLOPS = 2 * K * N * S
+
+F32 = mybir.dt.float32
+BF16 = mybir.dt.bfloat16
+I32 = mybir.dt.int32
+U32 = mybir.dt.uint32
+U16 = mybir.dt.uint16
+U8 = mybir.dt.uint8
+FP8X4 = mybir.dt.float8_e4m3fn_x4
+ALU = mybir.AluOpType
+ACT = mybir.ActivationFunctionType
+
+HALF = S // 2
+CHUNKS = ((0, 256), (256, 128), (384, 128))
+EXP_CAP = 2.0 ** 60
+
+
+def tile_picked_yseir_two_p_kernel(
+    tc, x_words, x_scales, w1, sus, inf, lat, mob, rate, offs, pos1, pos2, pos3, out
+):
+    nc = tc.nc
+    with ExitStack() as ctx:
+        lists = ctx.enter_context(tc.tile_pool(name="lists", bufs=1))
+        sb = ctx.enter_context(tc.tile_pool(name="sb", bufs=1))
+        ps = ctx.enter_context(tc.psum_pool(name="ps", bufs=1))
+
+        offs_t = lists.tile([P, S // 16], U16, name="offs_t")
+        pos_t = [lists.tile([P, S // 16], U16, name="pos_t%d" % d) for d in range(D)]
+
+        scale_tab = sb.tile([P, T], U8, name="scale_tab", tag="slot_a", align_bytes=64)
+        nc.gpsimd.memset(scale_tab[:].bitcast(I32), 0)
+        nc.sync.dma_start(offs_t[:], offs)
+        for r in range(4):
+            nc.scalar.dma_start(scale_tab[r:P:32, :].bitcast(I32), x_scales[0, r:16:4, :].bitcast(I32))
+        nc.sync.dma_start(pos_t[0][:], pos1)
+        w_raw = sb.tile([P, 4, N], F32, name="w_raw", tag="slot_b")
+        nc.sync.dma_start(w_raw[:], w1.rearrange("(p j) c -> p j c", j=4))
+        word_tab = sb.tile([P, T], U32, name="word_tab", tag="slot_c", align_bytes=64)
+        nc.sync.dma_start(word_tab[:].bitcast(I32), x_words[0].rearrange("p n t -> p (n t)").bitcast(I32))
+        nc.sync.dma_start(pos_t[1][:], pos2)
+        nc.sync.dma_start(pos_t[2][:], pos3)
+
+        ident = sb.tile([P, P], F32, name="ident")
+        make_identity(nc, ident[:])
+
+        x_sc = sb.tile([P, S], U8, name="x_sc", align_bytes=64)
+        nc.vector.tensor_copy(x_sc[:], scale_tab[:].indirect(offs_t[:]))
+
+        w_bf = sb.tile([P, N, 4], BF16, name="w_bf", tag="slot_d", align_bytes=64)
+        nc.scalar.activation(w_bf[:], w_raw[:].rearrange("p j c -> p c j"), ACT.Copy)
+        w_codes = sb.tile([P, N], U32, name="w_codes", align_bytes=64)
+        w_sc = sb.tile([P, N], U8, name="w_sc", align_bytes=64)
+        nc.vector.quantize_mx(
+            out=w_codes[:].bitcast(FP8X4), scales=w_sc[:], in_=w_bf[:].rearrange("p c j -> p (c j)")
+        )
+
+        inf_t = sb.tile([P, S], F32, name="inf_t", tag="slot_a", align_bytes=64)
+        nc.sync.dma_start(inf_t[:], inf)
+        lat_t = sb.tile([P, S], F32, name="lat_t", tag="slot_b")
+        nc.sync.dma_start(lat_t[:], lat)
+        rate_t = sb.tile([P, 1], F32, name="rate_t", tag="slot_d", align_bytes=64)
+        nc.sync.dma_start(rate_t[:], rate)
+
+        halves = [slice(h * HALF, (h + 1) * HALF) for h in range(2)]
+        y = []
+        ey = sb.tile([P, S], F32, name="ey")
+        for h in range(2):
+            x_codes = sb.tile([P, HALF], U32, name="x_codes%d" % h, align_bytes=64)
+            nc.vector.tensor_copy(x_codes[:], word_tab[:].indirect(offs_t[:, h * 16 : (h + 1) * 16]))
+            y_h = ps.tile([P, HALF], F32, name="y%d" % h, tag="bank%d" % h)
+            nc.tensor.matmul_mx(
+                out=y_h[:],
+                lhsT=w_codes[:].bitcast(FP8X4),
+                lhsT_scale=w_sc[:],
+                rhs=x_codes[:].bitcast(FP8X4),
+                rhs_scale=x_sc[:, halves[h]],
+                start=True,
+                stop=True,
+            )
+            nc.scalar.activation(ey[:, halves[h]], y_h[:], ACT.Exp)
+            y.append(y_h)
+
+        late = sb.tile([P, D + 1, S], F32, name="late", tag="slot_c", align_bytes=64)
+        for d in range(D):
+            nc.sync.dma_start(late[:, d, :], mob[d])
+        nc.sync.dma_start(late[:, D, :], sus)
+        mob_t = late
+        sus_t = late[:, D, :]
+
+        capped = sb.tile([P, S], F32, name="capped")
+        nc.vector.tensor_scalar(capped[:], ey[:], EXP_CAP, None, ALU.min)
+        rl = sb.tile([P, S], F32, name="rl")
+        nc.vector.tensor_scalar(rl[:], lat_t[:], rate_t[:], None, ALU.mult)
+        both = sb.tile([P, S], F32, name="both")
+        nc.vector.scalar_tensor_tensor(both[:], inf_t[:], 1.7, rl[:], ALU.mult, ALU.add)
+
+        def turn(bank, src, c0, width, start, stop):
+            blocks = width // P
+            for b in range(blocks):
+                nc.tensor.matmul(
+                    bank[:, b * P : (b + 1) * P],
+                    src[:, c0 + b * P : c0 + (b + 1) * P],
+                    ident[:],
+                    start=start and b == 0,
+                    stop=stop and b == blocks - 1,
+                    is_transpose=True,
+                )
+
+        acc1 = ps.tile([P, S], F32, name="acc1", tag="bank3")
+        turn(acc1, inf_t, 0, S, True, False)
+        acc2 = []
+        for c, (c0, width) in enumerate(CHUNKS):
+            a = ps.tile([P, width], F32, name="acc2_%d" % c, tag="bank%d" % (4 + c))
+            turn(a, both, c0, width, True, False)
+            acc2.append(a)
+
+        soft_raw = sb.tile([P, S], F32, name="soft_raw")
+        bi_tab = sb.tile([P, 2 * S], F32, name="bi_tab")
+        soft = bi_tab[:, S : 2 * S]
+        for h in range(2):
+            nc.scalar.activation(soft_raw[:, halves[h]], capped[:, halves[h]], ACT.Ln, bias=1.0)
+            nc.vector.tensor_tensor(soft[:, halves[h]], y[h][:], soft_raw[:, halves[h]], ALU.max)
+            nc.vector.scalar_tensor_tensor(
+                bi_tab[:, halves[h]], soft[:, halves[h]], 0.6, inf_t[:, halves[h]], ALU.mult, ALU.mult
+            )
+
+        soft_ps = ps.tile([P, S], F32, name="soft_ps", tag="bank2")
+        turn(soft_ps, soft, 0, S, True, True)
+        soft_tr = sb.tile([P, S], F32, name="soft_tr")
+        nc.scalar.activation(soft_tr[:], soft_ps[:], ACT.Copy)
+
+        for d in range(D):
+            term = sb.tile([P, S], F32, name="term1_%d" % d)
+            nc.vector.tensor_tensor(term[:], bi_tab[:].indirect(pos_t[d][:]), mob_t[:, d, :], ALU.mult)
+            turn(acc1, term, 0, S, False, d == D - 1)
+
+        b2_tab = sb.tile([P, S], F32, name="b2_tab")
+        nc.vector.scalar_tensor_tensor(b2_tab[:], soft, 0.6, both[:], ALU.mult, ALU.mult)
+
+        f1 = sb.tile([P, S], F32, name="f1")
+        nc.vector.tensor_tensor(f1[:], acc1[:], soft_tr[:], ALU.mult)
+        e1 = sb.tile([P, S], F32, name="e1")
+        nc.scalar.activation(e1[:], f1[:], ACT.Exp, scale=-0.6)
+        n1 = sb.tile([P, S], F32, name="n1")
+        nc.scalar.activation(n1[:], e1[:], ACT.Copy, scale=-1.0)
+        diff = []
+        for c, (c0, width) in enumerate(CHUNKS):
+            a = ps.tile([P, width], F32, name="diff%d" % c, tag="bank%d" % c)
+            turn(a, n1, c0, width, True, False)
+            diff.append(a)
+
+        def gather2(c):
+            c0, width = CHUNKS[c]
+            for d in range(D):
+                term = sb.tile([P, width], F32, name="term2_%d_%d" % (c, d))
+                nc.vector.tensor_tensor(
+                    term[:],
+                    b2_tab[:].indirect(pos_t[d][:, c0 // 16 : (c0 + width) // 16]),
+                    mob_t[:, d, c0 : c0 + width],
+                    ALU.mult,
+                )
+                turn(acc2[c], term, 0, width, False, d == D - 1)
+
+        def decay(c):
+            c0, width = CHUNKS[c]
+            f2 = sb.tile([P, width], F32, name="f2_%d" % c)
+            nc.vector.tensor_tensor(f2[:], acc2[c][:], soft_tr[:, c0 : c0 + width], ALU.mult)
+            e2 = sb.tile([P, width], F32, name="e2_%d" % c)
+            nc.scalar.activation(e2[:], f2[:], ACT.Exp, scale=-0.6)
+            turn(diff[c], e2, 0, width, False, True)
+
+        def finish(c):
+            c0, width = CHUNKS[c]
+            res = sb.tile([P, width], F32, name="res%d" % c)
+            nc.vector.scalar_tensor_tensor(
+                res[:], diff[c][:], -1.0, sus_t[:, c0 : c0 + width], ALU.mult, ALU.mult
+            )
+            nc.sync.dma_start(out[:, c0 : c0 + width], res[:])
+
+        gather2(0)
+        gather2(1)
+        decay(0)
+        gather2(2)
+        decay(1)
+        finish(0)
+        decay(2)
+        finish(1)
+        finish(2)

@@ -18,7 +18,7 @@ ALU = mybir.AluOpType
 ACT = mybir.ActivationFunctionType
 
 HALF = S // 2
-CHUNKS = ((0, 256), (256, 128), (384, 128))
+CHUNKS = ((0, 128), (128, 128), (256, 128), (384, 128))
 EXP_CAP = 2.0 ** 60
 
 
@@ -34,18 +34,32 @@ def tile_picked_yseir_two_p_kernel(
         offs_t = lists.tile([P, S // 16], U16, name="offs_t")
         pos_t = [lists.tile([P, S // 16], U16, name="pos_t%d" % d) for d in range(D)]
 
-        scale_tab = sb.tile([P, T], U8, name="scale_tab", tag="slot_a", align_bytes=64)
-        nc.gpsimd.memset(scale_tab[:].bitcast(I32), 0)
         nc.sync.dma_start(offs_t[:], offs)
+        scale_rows = sb.tile([P, T], U8, name="scale_rows", align_bytes=64)
         for r in range(4):
-            nc.scalar.dma_start(scale_tab[r:P:32, :].bitcast(I32), x_scales[0, r:16:4, :].bitcast(I32))
-        nc.sync.dma_start(pos_t[0][:], pos1)
-        w_raw = sb.tile([P, 4, N], F32, name="w_raw", tag="slot_b")
+            nc.sync.dma_start(scale_rows[r:P:32, :].bitcast(I32), x_scales[0, r:16:4, :].bitcast(I32))
+        w_raw = sb.tile([P, 4, N], F32, name="w_raw")
         nc.sync.dma_start(w_raw[:], w1.rearrange("(p j) c -> p j c", j=4))
-        word_tab = sb.tile([P, T], U32, name="word_tab", tag="slot_c", align_bytes=64)
+        word_tab = sb.tile([P, T], U32, name="word_tab", align_bytes=64)
         nc.sync.dma_start(word_tab[:].bitcast(I32), x_words[0].rearrange("p n t -> p (n t)").bitcast(I32))
-        nc.sync.dma_start(pos_t[1][:], pos2)
-        nc.sync.dma_start(pos_t[2][:], pos3)
+        inf_t = sb.tile([P, S], F32, name="inf_t")
+        nc.sync.dma_start(inf_t[:], inf)
+        lat_t = sb.tile([P, S], F32, name="lat_t")
+        nc.sync.dma_start(lat_t[:], lat)
+        rate_t = sb.tile([P, 1], F32, name="rate_t")
+        nc.sync.dma_start(rate_t[:], rate)
+        mob_t = [sb.tile([P, S], F32, name="mob_t%d" % d) for d in range(D)]
+        for d, pos in enumerate((pos1, pos2, pos3)):
+            nc.sync.dma_start(pos_t[d][:], pos)
+            nc.sync.dma_start(mob_t[d][:], mob[d])
+        sus_t = sb.tile([P, S], F32, name="sus_t")
+        nc.sync.dma_start(sus_t[:], sus)
+
+        scale_tab = sb.tile([P, T], U8, name="scale_tab", align_bytes=64)
+        nc.vector.memset(scale_tab[:].bitcast(I32), 0)
+        for q in range(4):
+            rows = slice(32 * q, 32 * q + 4)
+            nc.vector.tensor_copy(scale_tab[rows, :].bitcast(I32), scale_rows[rows, :].bitcast(I32))
 
         ident = sb.tile([P, P], F32, name="ident")
         make_identity(nc, ident[:])
@@ -53,20 +67,13 @@ def tile_picked_yseir_two_p_kernel(
         x_sc = sb.tile([P, S], U8, name="x_sc", align_bytes=64)
         nc.vector.tensor_copy(x_sc[:], scale_tab[:].indirect(offs_t[:]))
 
-        w_bf = sb.tile([P, N, 4], BF16, name="w_bf", tag="slot_d", align_bytes=64)
+        w_bf = sb.tile([P, N, 4], BF16, name="w_bf", align_bytes=64)
         nc.scalar.activation(w_bf[:], w_raw[:].rearrange("p j c -> p c j"), ACT.Copy)
         w_codes = sb.tile([P, N], U32, name="w_codes", align_bytes=64)
         w_sc = sb.tile([P, N], U8, name="w_sc", align_bytes=64)
         nc.vector.quantize_mx(
             out=w_codes[:].bitcast(FP8X4), scales=w_sc[:], in_=w_bf[:].rearrange("p c j -> p (c j)")
         )
-
-        inf_t = sb.tile([P, S], F32, name="inf_t", tag="slot_a", align_bytes=64)
-        nc.sync.dma_start(inf_t[:], inf)
-        lat_t = sb.tile([P, S], F32, name="lat_t", tag="slot_b")
-        nc.sync.dma_start(lat_t[:], lat)
-        rate_t = sb.tile([P, 1], F32, name="rate_t", tag="slot_d", align_bytes=64)
-        nc.sync.dma_start(rate_t[:], rate)
 
         halves = [slice(h * HALF, (h + 1) * HALF) for h in range(2)]
         y = []
@@ -87,19 +94,13 @@ def tile_picked_yseir_two_p_kernel(
             nc.scalar.activation(ey[:, halves[h]], y_h[:], ACT.Exp)
             y.append(y_h)
 
-        late = sb.tile([P, D + 1, S], F32, name="late", tag="slot_c", align_bytes=64)
-        for d in range(D):
-            nc.sync.dma_start(late[:, d, :], mob[d])
-        nc.sync.dma_start(late[:, D, :], sus)
-        mob_t = late
-        sus_t = late[:, D, :]
-
         capped = sb.tile([P, S], F32, name="capped")
         nc.vector.tensor_scalar(capped[:], ey[:], EXP_CAP, None, ALU.min)
         rl = sb.tile([P, S], F32, name="rl")
         nc.vector.tensor_scalar(rl[:], lat_t[:], rate_t[:], None, ALU.mult)
-        both = sb.tile([P, S], F32, name="both")
-        nc.vector.scalar_tensor_tensor(both[:], inf_t[:], 1.7, rl[:], ALU.mult, ALU.add)
+        b2_tab = sb.tile([P, 2 * S], F32, name="b2_tab")
+        both = b2_tab[:, S : 2 * S]
+        nc.vector.scalar_tensor_tensor(both, inf_t[:], 1.7, rl[:], ALU.mult, ALU.add)
 
         def turn(bank, src, c0, width, start, stop):
             blocks = width // P
@@ -127,9 +128,12 @@ def tile_picked_yseir_two_p_kernel(
         for h in range(2):
             nc.scalar.activation(soft_raw[:, halves[h]], capped[:, halves[h]], ACT.Ln, bias=1.0)
             nc.vector.tensor_tensor(soft[:, halves[h]], y[h][:], soft_raw[:, halves[h]], ALU.max)
+        for h in range(2):
             nc.vector.scalar_tensor_tensor(
                 bi_tab[:, halves[h]], soft[:, halves[h]], 0.6, inf_t[:, halves[h]], ALU.mult, ALU.mult
             )
+
+        nc.vector.scalar_tensor_tensor(b2_tab[:, 0:S], soft, 0.6, both, ALU.mult, ALU.mult)
 
         soft_ps = ps.tile([P, S], F32, name="soft_ps", tag="bank2")
         turn(soft_ps, soft, 0, S, True, True)
@@ -138,11 +142,21 @@ def tile_picked_yseir_two_p_kernel(
 
         for d in range(D):
             term = sb.tile([P, S], F32, name="term1_%d" % d)
-            nc.vector.tensor_tensor(term[:], bi_tab[:].indirect(pos_t[d][:]), mob_t[:, d, :], ALU.mult)
+            nc.vector.tensor_tensor(term[:], bi_tab[:].indirect(pos_t[d][:]), mob_t[d][:], ALU.mult)
             turn(acc1, term, 0, S, False, d == D - 1)
 
-        b2_tab = sb.tile([P, S], F32, name="b2_tab")
-        nc.vector.scalar_tensor_tensor(b2_tab[:], soft, 0.6, both[:], ALU.mult, ALU.mult)
+        def gather2(d, c0, width):
+            term = sb.tile([P, width], F32, name="term2_%d_%d" % (d, c0))
+            nc.vector.tensor_tensor(
+                term[:],
+                b2_tab[:].indirect(pos_t[d][:, c0 // 16 : (c0 + width) // 16]),
+                mob_t[d][:, c0 : c0 + width],
+                ALU.mult,
+            )
+            for b in range(width // P):
+                turn(acc2[c0 // P + b], term, b * P, P, False, d == D - 1)
+
+        gather2(0, 0, S)
 
         f1 = sb.tile([P, S], F32, name="f1")
         nc.vector.tensor_tensor(f1[:], acc1[:], soft_tr[:], ALU.mult)
@@ -150,46 +164,27 @@ def tile_picked_yseir_two_p_kernel(
         nc.scalar.activation(e1[:], f1[:], ACT.Exp, scale=-0.6)
         n1 = sb.tile([P, S], F32, name="n1")
         nc.scalar.activation(n1[:], e1[:], ACT.Copy, scale=-1.0)
+
+        gather2(1, 0, S)
+
         diff = []
         for c, (c0, width) in enumerate(CHUNKS):
             a = ps.tile([P, width], F32, name="diff%d" % c, tag="bank%d" % c)
             turn(a, n1, c0, width, True, False)
             diff.append(a)
 
-        def gather2(c):
-            c0, width = CHUNKS[c]
-            for d in range(D):
-                term = sb.tile([P, width], F32, name="term2_%d_%d" % (c, d))
-                nc.vector.tensor_tensor(
-                    term[:],
-                    b2_tab[:].indirect(pos_t[d][:, c0 // 16 : (c0 + width) // 16]),
-                    mob_t[:, d, c0 : c0 + width],
-                    ALU.mult,
-                )
-                turn(acc2[c], term, 0, width, False, d == D - 1)
-
-        def decay(c):
-            c0, width = CHUNKS[c]
+        for c0, width in CHUNKS:
+            gather2(2, c0, width)
+        for c, (c0, width) in enumerate(CHUNKS):
             f2 = sb.tile([P, width], F32, name="f2_%d" % c)
             nc.vector.tensor_tensor(f2[:], acc2[c][:], soft_tr[:, c0 : c0 + width], ALU.mult)
             e2 = sb.tile([P, width], F32, name="e2_%d" % c)
             nc.scalar.activation(e2[:], f2[:], ACT.Exp, scale=-0.6)
             turn(diff[c], e2, 0, width, False, True)
 
-        def finish(c):
-            c0, width = CHUNKS[c]
-            res = sb.tile([P, width], F32, name="res%d" % c)
+        res = sb.tile([P, S], F32, name="res")
+        for c, (c0, width) in enumerate(CHUNKS):
             nc.vector.scalar_tensor_tensor(
-                res[:], diff[c][:], -1.0, sus_t[:, c0 : c0 + width], ALU.mult, ALU.mult
+                res[:, c0 : c0 + width], diff[c][:], -1.0, sus_t[:, c0 : c0 + width], ALU.mult, ALU.mult
             )
-            nc.sync.dma_start(out[:, c0 : c0 + width], res[:])
-
-        gather2(0)
-        gather2(1)
-        decay(0)
-        gather2(2)
-        decay(1)
-        finish(0)
-        decay(2)
-        finish(1)
-        finish(2)
+            nc.sync.dma_start(out[:, c0 : c0 + width], res[:, c0 : c0 + width])

@@ -1,3 +1,4 @@
+import math
 from contextlib import ExitStack
 
 import concourse.mybir as mybir
@@ -20,6 +21,8 @@ ACT = mybir.ActivationFunctionType
 HALF = S // 2
 CHUNKS = ((0, 128), (128, 128), (256, 128), (384, 128))
 EXP_CAP = 2.0 ** 60
+Y_CAP = math.log(EXP_CAP)
+PIECES = ((0, 256), (256, 128), (384, 128))
 
 
 def tile_picked_yseir_two_p_kernel(
@@ -42,12 +45,12 @@ def tile_picked_yseir_two_p_kernel(
         nc.sync.dma_start(w_raw[:], w1.rearrange("(p j) c -> p j c", j=4))
         word_tab = sb.tile([P, T], U32, name="word_tab", align_bytes=64)
         nc.sync.dma_start(word_tab[:].bitcast(I32), x_words[0].rearrange("p n t -> p (n t)").bitcast(I32))
-        inf_t = sb.tile([P, S], F32, name="inf_t")
-        nc.sync.dma_start(inf_t[:], inf)
-        lat_t = sb.tile([P, S], F32, name="lat_t")
-        nc.sync.dma_start(lat_t[:], lat)
         rate_t = sb.tile([P, 1], F32, name="rate_t")
         nc.sync.dma_start(rate_t[:], rate)
+        lat_t = sb.tile([P, S], F32, name="lat_t")
+        nc.sync.dma_start(lat_t[:], lat)
+        inf_t = sb.tile([P, S], F32, name="inf_t")
+        nc.sync.dma_start(inf_t[:], inf)
         mob_t = [sb.tile([P, S], F32, name="mob_t%d" % d) for d in range(D)]
         for d, pos in enumerate((pos1, pos2, pos3)):
             nc.sync.dma_start(pos_t[d][:], pos)
@@ -76,31 +79,41 @@ def tile_picked_yseir_two_p_kernel(
         )
 
         halves = [slice(h * HALF, (h + 1) * HALF) for h in range(2)]
+        x_codes = sb.tile([P, S], U32, name="x_codes", align_bytes=64)
+        for h in range(2):
+            nc.vector.tensor_copy(x_codes[:, halves[h]], word_tab[:].indirect(offs_t[:, h * 16 : (h + 1) * 16]))
         y = []
         ey = sb.tile([P, S], F32, name="ey")
-        for h in range(2):
-            x_codes = sb.tile([P, HALF], U32, name="x_codes%d" % h, align_bytes=64)
-            nc.vector.tensor_copy(x_codes[:], word_tab[:].indirect(offs_t[:, h * 16 : (h + 1) * 16]))
-            y_h = ps.tile([P, HALF], F32, name="y%d" % h, tag="bank%d" % h)
+        for i, (c0, width) in enumerate(PIECES):
+            cols = slice(c0, c0 + width)
+            y_i = ps.tile([P, width], F32, name="y%d" % i, tag="bank%d" % i)
             nc.tensor.matmul_mx(
-                out=y_h[:],
+                out=y_i[:],
                 lhsT=w_codes[:].bitcast(FP8X4),
                 lhsT_scale=w_sc[:],
-                rhs=x_codes[:].bitcast(FP8X4),
-                rhs_scale=x_sc[:, halves[h]],
+                rhs=x_codes[:, cols].bitcast(FP8X4),
+                rhs_scale=x_sc[:, cols],
                 start=True,
                 stop=True,
             )
-            nc.scalar.activation(ey[:, halves[h]], y_h[:], ACT.Exp)
-            y.append(y_h)
+            nc.scalar.activation(ey[:, cols], y_i[:], ACT.Exp)
+            y.append(y_i)
 
-        capped = sb.tile([P, S], F32, name="capped")
-        nc.vector.tensor_scalar(capped[:], ey[:], EXP_CAP, None, ALU.min)
         rl = sb.tile([P, S], F32, name="rl")
         nc.vector.tensor_scalar(rl[:], lat_t[:], rate_t[:], None, ALU.mult)
+        both = sb.tile([P, S], F32, name="both")
+        nc.vector.scalar_tensor_tensor(both[:], inf_t[:], 1.7, rl[:], ALU.mult, ALU.add)
+        excess = sb.tile([P, S], F32, name="excess")
+        for i, (c0, width) in enumerate(PIECES):
+            nc.vector.tensor_scalar(excess[:, c0 : c0 + width], y[i][:], -Y_CAP, 0.0, ALU.add, ALU.max)
+        capped = sb.tile([P, S], F32, name="capped")
+        nc.vector.tensor_scalar(capped[:], ey[:], EXP_CAP, None, ALU.min)
+        bi_tab = sb.tile([P, 2 * S], F32, name="bi_tab")
         b2_tab = sb.tile([P, 2 * S], F32, name="b2_tab")
-        both = b2_tab[:, S : 2 * S]
-        nc.vector.scalar_tensor_tensor(both, inf_t[:], 1.7, rl[:], ALU.mult, ALU.add)
+        inf_up = bi_tab[:, S : 2 * S]
+        both_up = b2_tab[:, S : 2 * S]
+        nc.vector.scalar_tensor_tensor(inf_up, excess[:], Y_CAP, inf_t[:], ALU.add, ALU.mult)
+        nc.vector.scalar_tensor_tensor(both_up, excess[:], Y_CAP, both[:], ALU.add, ALU.mult)
 
         def turn(bank, src, c0, width, start, stop):
             blocks = width // P
@@ -114,29 +127,25 @@ def tile_picked_yseir_two_p_kernel(
                     is_transpose=True,
                 )
 
-        acc1 = ps.tile([P, S], F32, name="acc1", tag="bank3")
+        acc1 = ps.tile([P, S], F32, name="acc1", tag="bank0")
         turn(acc1, inf_t, 0, S, True, False)
+        soft_ps = ps.tile([P, S], F32, name="soft_ps", tag="bank4")
+        turn(soft_ps, excess, 0, S, True, False)
         acc2 = []
         for c, (c0, width) in enumerate(CHUNKS):
-            a = ps.tile([P, width], F32, name="acc2_%d" % c, tag="bank%d" % (4 + c))
+            a = ps.tile([P, width], F32, name="acc2_%d" % c, tag="bank%d" % (5, 1, 2, 3)[c])
             turn(a, both, c0, width, True, False)
             acc2.append(a)
 
-        soft_raw = sb.tile([P, S], F32, name="soft_raw")
-        bi_tab = sb.tile([P, 2 * S], F32, name="bi_tab")
-        soft = bi_tab[:, S : 2 * S]
+        soft_low = sb.tile([P, S], F32, name="soft_low")
         for h in range(2):
-            nc.scalar.activation(soft_raw[:, halves[h]], capped[:, halves[h]], ACT.Ln, bias=1.0)
-            nc.vector.tensor_tensor(soft[:, halves[h]], y[h][:], soft_raw[:, halves[h]], ALU.max)
-        for h in range(2):
+            nc.scalar.activation(soft_low[:, halves[h]], capped[:, halves[h]], ACT.Ln, bias=1.0)
             nc.vector.scalar_tensor_tensor(
-                bi_tab[:, halves[h]], soft[:, halves[h]], 0.6, inf_t[:, halves[h]], ALU.mult, ALU.mult
+                bi_tab[:, halves[h]], soft_low[:, halves[h]], 0.6 / Y_CAP, inf_up[:, halves[h]], ALU.mult, ALU.mult
             )
+        nc.vector.scalar_tensor_tensor(b2_tab[:, 0:S], soft_low[:], 0.6 / Y_CAP, both_up, ALU.mult, ALU.mult)
 
-        nc.vector.scalar_tensor_tensor(b2_tab[:, 0:S], soft, 0.6, both, ALU.mult, ALU.mult)
-
-        soft_ps = ps.tile([P, S], F32, name="soft_ps", tag="bank2")
-        turn(soft_ps, soft, 0, S, True, True)
+        turn(soft_ps, soft_low, 0, S, False, True)
         soft_tr = sb.tile([P, S], F32, name="soft_tr")
         nc.scalar.activation(soft_tr[:], soft_ps[:], ACT.Copy)
 
@@ -169,7 +178,7 @@ def tile_picked_yseir_two_p_kernel(
 
         diff = []
         for c, (c0, width) in enumerate(CHUNKS):
-            a = ps.tile([P, width], F32, name="diff%d" % c, tag="bank%d" % c)
+            a = ps.tile([P, width], F32, name="diff%d" % c, tag="bank%d" % (4, 0, 6, 7)[c])
             turn(a, n1, c0, width, True, False)
             diff.append(a)
 

import math
from contextlib import ExitStack

import concourse.mybir as mybir
from concourse.masks import make_identity

K, T, S, N, D = 512, 2048, 512, 128, 3
P = 128
FLOPS = 2 * K * N * S

F32 = mybir.dt.float32
BF16 = mybir.dt.bfloat16
I32 = mybir.dt.int32
U32 = mybir.dt.uint32
U16 = mybir.dt.uint16
U8 = mybir.dt.uint8
FP8X4 = mybir.dt.float8_e4m3fn_x4
ALU = mybir.AluOpType
ACT = mybir.ActivationFunctionType

HALF = S // 2
CHUNKS = ((0, 128), (128, 128), (256, 128), (384, 128))
EXP_CAP = 2.0 ** 60
Y_CAP = math.log(EXP_CAP)
PIECES = ((0, 256), (256, 128), (384, 128))


def tile_picked_yseir_two_p_kernel(
    tc, x_words, x_scales, w1, sus, inf, lat, mob, rate, offs, pos1, pos2, pos3, out
):
    nc = tc.nc
    with ExitStack() as ctx:
        lists = ctx.enter_context(tc.tile_pool(name="lists", bufs=1))
        sb = ctx.enter_context(tc.tile_pool(name="sb", bufs=1))
        ps = ctx.enter_context(tc.psum_pool(name="ps", bufs=1))

        offs_t = lists.tile([P, S // 16], U16, name="offs_t")
        pos_t = [lists.tile([P, S // 16], U16, name="pos_t%d" % d) for d in range(D)]

        nc.sync.dma_start(offs_t[:], offs)
        scale_rows = sb.tile([P, T], U8, name="scale_rows", align_bytes=64)
        for r in range(4):
            nc.sync.dma_start(scale_rows[r:P:32, :].bitcast(I32), x_scales[0, r:16:4, :].bitcast(I32))
        w_raw = sb.tile([P, 4, N], F32, name="w_raw")
        nc.sync.dma_start(w_raw[:], w1.rearrange("(p j) c -> p j c", j=4))
        word_tab = sb.tile([P, T], U32, name="word_tab", align_bytes=64)
        nc.sync.dma_start(word_tab[:].bitcast(I32), x_words[0].rearrange("p n t -> p (n t)").bitcast(I32))
        rate_t = sb.tile([P, 1], F32, name="rate_t")
        nc.sync.dma_start(rate_t[:], rate)
        lat_t = sb.tile([P, S], F32, name="lat_t")
        nc.sync.dma_start(lat_t[:], lat)
        inf_t = sb.tile([P, S], F32, name="inf_t")
        nc.sync.dma_start(inf_t[:], inf)
        mob_t = [sb.tile([P, S], F32, name="mob_t%d" % d) for d in range(D)]
        for d, pos in enumerate((pos1, pos2, pos3)):
            nc.sync.dma_start(pos_t[d][:], pos)
            nc.sync.dma_start(mob_t[d][:], mob[d])
        sus_t = sb.tile([P, S], F32, name="sus_t")
        nc.sync.dma_start(sus_t[:], sus)

        scale_tab = sb.tile([P, T], U8, name="scale_tab", align_bytes=64)
        nc.vector.memset(scale_tab[:].bitcast(I32), 0)
        for q in range(4):
            rows = slice(32 * q, 32 * q + 4)
            nc.vector.tensor_copy(scale_tab[rows, :].bitcast(I32), scale_rows[rows, :].bitcast(I32))

        ident = sb.tile([P, P], F32, name="ident")
        make_identity(nc, ident[:])

        x_sc = sb.tile([P, S], U8, name="x_sc", align_bytes=64)
        nc.vector.tensor_copy(x_sc[:], scale_tab[:].indirect(offs_t[:]))

        w_bf = sb.tile([P, N, 4], BF16, name="w_bf", align_bytes=64)
        nc.scalar.activation(w_bf[:], w_raw[:].rearrange("p j c -> p c j"), ACT.Copy)
        w_codes = sb.tile([P, N], U32, name="w_codes", align_bytes=64)
        w_sc = sb.tile([P, N], U8, name="w_sc", align_bytes=64)
        nc.vector.quantize_mx(
            out=w_codes[:].bitcast(FP8X4), scales=w_sc[:], in_=w_bf[:].rearrange("p c j -> p (c j)")
        )

        halves = [slice(h * HALF, (h + 1) * HALF) for h in range(2)]
        x_codes = sb.tile([P, S], U32, name="x_codes", align_bytes=64)
        for h in range(2):
            nc.vector.tensor_copy(x_codes[:, halves[h]], word_tab[:].indirect(offs_t[:, h * 16 : (h + 1) * 16]))
        y = []
        ey = sb.tile([P, S], F32, name="ey")
        for i, (c0, width) in enumerate(PIECES):
            cols = slice(c0, c0 + width)
            y_i = ps.tile([P, width], F32, name="y%d" % i, tag="bank%d" % i)
            nc.tensor.matmul_mx(
                out=y_i[:],
                lhsT=w_codes[:].bitcast(FP8X4),
                lhsT_scale=w_sc[:],
                rhs=x_codes[:, cols].bitcast(FP8X4),
                rhs_scale=x_sc[:, cols],
                start=True,
                stop=True,
            )
            nc.scalar.activation(ey[:, cols], y_i[:], ACT.Exp)
            y.append(y_i)

        rl = sb.tile([P, S], F32, name="rl")
        nc.vector.tensor_scalar(rl[:], lat_t[:], rate_t[:], None, ALU.mult)
        both = sb.tile([P, S], F32, name="both")
        nc.vector.scalar_tensor_tensor(both[:], inf_t[:], 1.7, rl[:], ALU.mult, ALU.add)
        excess = sb.tile([P, S], F32, name="excess")
        for i, (c0, width) in enumerate(PIECES):
            nc.vector.tensor_scalar(excess[:, c0 : c0 + width], y[i][:], -Y_CAP, 0.0, ALU.add, ALU.max)
        capped = sb.tile([P, S], F32, name="capped")
        nc.vector.tensor_scalar(capped[:], ey[:], EXP_CAP, None, ALU.min)
        bi_tab = sb.tile([P, 2 * S], F32, name="bi_tab")
        b2_tab = sb.tile([P, 2 * S], F32, name="b2_tab")
        inf_up = bi_tab[:, S : 2 * S]
        both_up = b2_tab[:, S : 2 * S]
        nc.vector.scalar_tensor_tensor(inf_up, excess[:], Y_CAP, inf_t[:], ALU.add, ALU.mult)
        nc.vector.scalar_tensor_tensor(both_up, excess[:], Y_CAP, both[:], ALU.add, ALU.mult)

        def turn(bank, src, c0, width, start, stop):
            blocks = width // P
            for b in range(blocks):
                nc.tensor.matmul(
                    bank[:, b * P : (b + 1) * P],
                    src[:, c0 + b * P : c0 + (b + 1) * P],
                    ident[:],
                    start=start and b == 0,
                    stop=stop and b == blocks - 1,
                    is_transpose=True,
                )

        acc1 = ps.tile([P, S], F32, name="acc1", tag="bank0")
        turn(acc1, inf_t, 0, S, True, False)
        soft_ps = ps.tile([P, S], F32, name="soft_ps", tag="bank4")
        turn(soft_ps, excess, 0, S, True, False)
        acc2 = []
        for c, (c0, width) in enumerate(CHUNKS):
            a = ps.tile([P, width], F32, name="acc2_%d" % c, tag="bank%d" % (5, 1, 2, 3)[c])
            turn(a, both, c0, width, True, False)
            acc2.append(a)

        soft_low = sb.tile([P, S], F32, name="soft_low")
        for h in range(2):
            nc.scalar.activation(soft_low[:, halves[h]], capped[:, halves[h]], ACT.Ln, bias=1.0)
            nc.vector.scalar_tensor_tensor(
                bi_tab[:, halves[h]], soft_low[:, halves[h]], 0.6 / Y_CAP, inf_up[:, halves[h]], ALU.mult, ALU.mult
            )
        nc.vector.scalar_tensor_tensor(b2_tab[:, 0:S], soft_low[:], 0.6 / Y_CAP, both_up, ALU.mult, ALU.mult)

        turn(soft_ps, soft_low, 0, S, False, True)
        soft_tr = sb.tile([P, S], F32, name="soft_tr")
        nc.scalar.activation(soft_tr[:], soft_ps[:], ACT.Copy)

        for d in range(D):
            term = sb.tile([P, S], F32, name="term1_%d" % d)
            nc.vector.tensor_tensor(term[:], bi_tab[:].indirect(pos_t[d][:]), mob_t[d][:], ALU.mult)
            turn(acc1, term, 0, S, False, d == D - 1)

        def gather2(d, c0, width):
            term = sb.tile([P, width], F32, name="term2_%d_%d" % (d, c0))
            nc.vector.tensor_tensor(
                term[:],
                b2_tab[:].indirect(pos_t[d][:, c0 // 16 : (c0 + width) // 16]),
                mob_t[d][:, c0 : c0 + width],
                ALU.mult,
            )
            for b in range(width // P):
                turn(acc2[c0 // P + b], term, b * P, P, False, d == D - 1)

        gather2(0, 0, S)

        f1 = sb.tile([P, S], F32, name="f1")
        nc.vector.tensor_tensor(f1[:], acc1[:], soft_tr[:], ALU.mult)
        e1 = sb.tile([P, S], F32, name="e1")
        nc.scalar.activation(e1[:], f1[:], ACT.Exp, scale=-0.6)
        n1 = sb.tile([P, S], F32, name="n1")
        nc.scalar.activation(n1[:], e1[:], ACT.Copy, scale=-1.0)

        gather2(1, 0, S)

        diff = []
        for c, (c0, width) in enumerate(CHUNKS):
            a = ps.tile([P, width], F32, name="diff%d" % c, tag="bank%d" % (4, 0, 6, 7)[c])
            turn(a, n1, c0, width, True, False)
            diff.append(a)

        for c0, width in CHUNKS:
            gather2(2, c0, width)
        for c, (c0, width) in enumerate(CHUNKS):
            f2 = sb.tile([P, width], F32, name="f2_%d" % c)
            nc.vector.tensor_tensor(f2[:], acc2[c][:], soft_tr[:, c0 : c0 + width], ALU.mult)
            e2 = sb.tile([P, width], F32, name="e2_%d" % c)
            nc.scalar.activation(e2[:], f2[:], ACT.Exp, scale=-0.6)
            turn(diff[c], e2, 0, width, False, True)

        res = sb.tile([P, S], F32, name="res")
        for c, (c0, width) in enumerate(CHUNKS):
            nc.vector.scalar_tensor_tensor(
                res[:, c0 : c0 + width], diff[c][:], -1.0, sus_t[:, c0 : c0 + width], ALU.mult, ALU.mult
            )
            nc.sync.dma_start(out[:, c0 : c0 + width], res[:, c0 : c0 + width])
